import numpy as np
import ml_dtypes


def mxq(x, axis, fmt="e4m3"):
    dtype, down = {"e4m3": (ml_dtypes.float8_e4m3fn, 7), "e5m2": (ml_dtypes.float8_e5m2, 14)}[fmt]
    v = np.moveaxis(np.asarray(x, np.float32).astype(ml_dtypes.bfloat16).astype(np.float64), axis, -1)
    blocks = v.reshape(v.shape[:-1] + (-1, 32))
    amax = np.abs(blocks).max(-1, keepdims=True)
    byte = np.maximum(np.where(amax > 0, np.frexp(amax)[1] - 1 + 127, 0) - down, 1)
    scale = np.exp2(byte - 127.0)
    codes = (blocks / scale).astype(np.float32).astype(dtype).astype(np.float64)
    return np.moveaxis((codes * scale).reshape(v.shape), -1, axis)


WIDE = False


def mx_kscale(k):
    if not WIDE:
        return np.ones(k)
    levels = np.array([30, -30])
    if k % 512:
        return np.exp2(np.random.permutation(np.resize(levels, k // 32))).repeat(32)
    a = np.empty((k // 512, 16))
    for p in range(k // 512):
        a[p, :8] = np.random.permutation(np.resize(levels, 8))
        for g in range(8):
            far = levels[np.abs(levels - a[p, g]) >= 10]
            a[p, g + 8] = far[np.random.randint(len(far))]
    return np.exp2(a.ravel()).repeat(32)


def f64(x):
    return np.asarray(x).astype(np.float64)


def striped(idx):
    return np.tile(np.asarray(idx).reshape(-1, 16).T, (8, 1)).astype(np.uint16)


def unstriped(offs):
    return offs[:16].T.reshape(-1).astype(np.int64)


E2M1 = np.array([0.0, 0.5, 1.0, 1.5, 2.0, 3.0, 4.0, 6.0, -0.0, -0.5, -1.0, -1.5, -2.0, -3.0, -4.0, -6.0])


def pack_weight(w, fmt):
    k, n = w.shape
    w = f64(np.asarray(w, np.float32).astype(ml_dtypes.bfloat16)).reshape(k // 32, 32, n)
    amax = np.abs(w).max(1)
    if fmt in ("e4m3", "e5m2"):
        byte = np.frexp(amax)[1] - 1 + 127 - (7 if fmt == "e4m3" else 14)
    else:
        mant, ex = np.frexp(amax / 6.0)
        byte = np.where(mant > 0.5, ex, ex - 1) + 127
    byte = np.clip(np.where(amax > 0, byte, 1), 1, 254)
    scaled = (w * np.exp2(127.0 - byte)[:, None, :]).reshape(k, n).astype(np.float32)
    by_word = np.ascontiguousarray(scaled.reshape(k // 512, 128, 4, n).transpose(0, 1, 3, 2))
    if fmt in ("e4m3", "e5m2"):
        words = by_word.astype(ml_dtypes.float8_e4m3fn if fmt == "e4m3" else ml_dtypes.float8_e5m2).view(np.uint8)
    else:
        c = by_word.astype(ml_dtypes.float4_e2m1fn).view(np.uint8) & 0xF
        words = (c[..., 0::2] | (c[..., 1::2] << 4)).reshape(k // 512, 128, 2 * n)
    return np.ascontiguousarray(words), np.ascontiguousarray(byte.astype(np.uint8).reshape(k // 512, 16, n))


def unpack_weight(words, scales, fmt):
    g, _, n = scales.shape
    words = np.ascontiguousarray(words).reshape(g, 128, n, -1)
    if fmt in ("e4m3", "e5m2"):
        vals = words.view(ml_dtypes.float8_e4m3fn if fmt == "e4m3" else ml_dtypes.float8_e5m2).astype(np.float64)
    else:
        nib = np.empty((g, 128, n, 4), np.uint8)
        nib[..., 0::2] = words & 0xF
        nib[..., 1::2] = words >> 4
        vals = E2M1[nib]
    vals = vals * np.repeat(np.exp2(scales.astype(np.float64) - 127.0), 8, axis=1)[..., None]
    return vals.transpose(0, 1, 3, 2).reshape(g * 512, n)


def sigmoid(v):
    return 1.0 / (1.0 + np.exp(-v))


def sgn(shape):
    return np.random.uniform(0.5, 2.0, shape) * np.where(np.random.standard_normal(shape) < 0, -1.0, 1.0)


K, T, J, R, N, U, E = 512, 2048, 256, 512, 256, 128, 512


def setup_inputs():
    n = np.random.standard_normal
    idx = np.random.permutation(T)[:J]
    idx2 = np.random.permutation(T)[:J]
    idx3 = np.random.permutation(J)[:U]
    idx4 = np.random.permutation(J)[:U]
    idx5 = np.random.permutation(E)[:U]
    idx6 = np.random.permutation(E)[:J]
    fk = mx_kscale(K)
    fr = mx_kscale(R)
    xtp = pack_weight(n((K, T)) / fk[:, None], "e5m2")
    wp = pack_weight(n((K, R)) * 1 / np.sqrt(K) * fk[:, None] * fr, "e2m1")
    w2p = pack_weight(n((K, R)) * 1 / np.sqrt(K) * fk[:, None] * fr, "e4m3")
    wbp = pack_weight(n((R, N)) * 1 / np.sqrt(R) / fr[:, None], "e2m1")
    wcp = pack_weight(n((R, N)) * 1 / np.sqrt(R) / fr[:, None], "e4m3")
    return {
        "xt_words": xtp[0],
        "xt_scales": xtp[1],
        "w_words": wp[0],
        "w_scales": wp[1],
        "w2_words": w2p[0],
        "w2_scales": w2p[1],
        "wb_words": wbp[0],
        "wb_scales": wbp[1],
        "wc_words": wcp[0],
        "wc_scales": wcp[1],
        "so": (np.random.uniform(0.5, 1.6, (N, 1))).astype(np.float32),
        "sp": (sgn((N, 1))).astype(np.float32),
        "bo": (np.random.uniform(-2.0, 2.0, (N, 1))).astype(np.float32),
        "offs": striped(idx),
        "offs2": striped(idx2),
        "offs3": striped(idx3),
        "offs4": striped(idx4),
        "offs5": striped(idx5),
        "offs6": striped(idx6),
    }


def reference(xt_words, xt_scales, w_words, w_scales, w2_words, w2_scales, wb_words, wb_scales, wc_words, wc_scales, so, sp, bo, offs, offs2, offs3, offs4, offs5, offs6):
    idx = unstriped(offs)
    idx2 = unstriped(offs2)
    idx3 = unstriped(offs3)
    idx4 = unstriped(offs4)
    idx5 = unstriped(offs5)
    idx6 = unstriped(offs6)
    xtu = unpack_weight(xt_words, xt_scales, "e5m2")
    wu = unpack_weight(w_words, w_scales, "e2m1")
    w2u = unpack_weight(w2_words, w2_scales, "e4m3")
    wbu = unpack_weight(wb_words, wb_scales, "e2m1")
    wcu = unpack_weight(wc_words, wc_scales, "e4m3")
    xtidxg = xtu[:, idx]
    a = wu.T @ xtidxg
    xtidx2g = xtu[:, idx2]
    b = w2u.T @ xtidx2g
    hid = np.abs(a - b)
    hidq = mxq(hid, 0, "e4m3")
    p = wbu.T @ hidq
    q = wcu.T @ hidq
    m0 = p[:, idx3] * f64(so) * sigmoid(p[:, idx4] * f64(sp) + f64(bo))
    pw = np.zeros((N, E))
    pw[:, idx5] = m0
    pv = np.zeros((N, E))
    pv[:, idx6] = q
    y = pw + pv
    return y

@@ -1,0 +1,223 @@
+from contextlib import ExitStack
+
+import concourse.mybir as mybir
+
+K, T, J, R, N, U, E = 512, 2048, 256, 512, 256, 128, 512
+FLOPS = 2 * (2 * K * R * J + 2 * R * N * J)
+
+F32 = mybir.dt.float32
+BF16 = mybir.dt.bfloat16
+I32 = mybir.dt.int32
+U32 = mybir.dt.uint32
+U16 = mybir.dt.uint16
+U8 = mybir.dt.uint8
+E4M3 = mybir.dt.float8_e4m3fn_x4
+E5M2 = mybir.dt.float8_e5m2_x4
+E2M1 = mybir.dt.float4_e2m1fn_x4
+ACT = mybir.ActivationFunctionType
+ALU = mybir.AluOpType
+
+P = 128
+PACK = 4
+HALF = J // 2
+LIST_COLS = HALF // 16
+
+
+def tile_list_outcomegatedpages_ahead_kernel(
+    tc, xt_words, xt_scales, w_words, w_scales, w2_words, w2_scales, wb_words, wb_scales, wc_words, wc_scales,
+    so, sp, bo, offs, offs2, offs3, offs4, offs5, offs6, out,
+):
+    nc = tc.nc
+    with ExitStack() as ctx:
+        lists = ctx.enter_context(tc.tile_pool(name="lists", bufs=1))
+        sb = ctx.enter_context(tc.tile_pool(name="sb", bufs=1))
+        psum = ctx.enter_context(tc.psum_pool(name="psum", bufs=1))
+
+        def tile(name, shape, dtype):
+            return sb.tile(shape, dtype, name=name, align_bytes=64)
+
+        def load_list(name, src):
+            t = lists.tile(list(src.shape), U16, name=name)
+            nc.sync.dma_start(t[:], src)
+            return t
+
+        def load_plane(queue, plane, scales):
+            for q in range(4):
+                queue.dma_start(plane[32 * q : 32 * q + 4, :].bitcast(I32), scales[0, 4 * q : 4 * q + 4, :].bitcast(I32))
+
+        x_plane = tile("x_plane", [P, T], U8)
+        nc.gpsimd.memset(x_plane[:].bitcast(I32), 0)
+        warm_in = tile("warm_in", [P, 1], F32)
+        warm_out = tile("warm_out", [P, 1], F32)
+        nc.vector.memset(warm_in[:], 0.0)
+        nc.scalar.activation(warm_out[:], warm_in[:], ACT.Sigmoid)
+        load_plane(nc.scalar, x_plane, xt_scales)
+
+        w_stage = tile("w_stage", [4, 4, 2 * R], U8)
+        for i, scales in enumerate((w_scales, w2_scales)):
+            nc.sync.dma_start(
+                w_stage[:, :, i * R : (i + 1) * R].bitcast(I32),
+                scales[0].rearrange("(q r) n -> r q n", r=4).bitcast(I32),
+            )
+        list1 = load_list("list1", offs)
+        w_raw = tile("w_raw", [P, 2 * R], U8)
+        nc.gpsimd.dma_start(w_raw[:].bitcast(I32), w_words[0].bitcast(I32))
+        x_words = tile("x_words", [P, T], U32)
+        nc.sync.dma_start(x_words[:].bitcast(I32), xt_words[0].rearrange("p t r -> p (t r)").bitcast(I32))
+        list2 = load_list("list2", offs2)
+        w2_raw = tile("w2_raw", [P, R], U32)
+        nc.sync.dma_start(w2_raw[:].bitcast(I32), w2_words[0].rearrange("p n r -> p (n r)").bitcast(I32))
+
+        w_planes_raw = tile("w_planes_raw", [P, 2 * R], U8)
+        nc.vector.memset(w_planes_raw[:].bitcast(I32), 0)
+        wb_plane = tile("wb_plane", [P, N], U8)
+        wc_plane = tile("wc_plane", [P, N], U8)
+        nc.vector.memset(wc_plane[:].bitcast(I32), 0)
+        nc.vector.memset(wb_plane[:].bitcast(I32), 0)
+        wb_codes = tile("wb_codes", [P, 2 * N], U8)
+        nc.sync.dma_start(wb_codes[:].bitcast(I32), wb_words[0].bitcast(I32))
+        wc_codes = tile("wc_codes", [P, N], U32)
+        nc.sync.dma_start(wc_codes[:].bitcast(I32), wc_words[0].rearrange("p n r -> p (n r)").bitcast(I32))
+        load_plane(nc.sync, wb_plane, wb_scales)
+        load_plane(nc.gpsimd, wc_plane, wc_scales)
+        list6 = load_list("list6", offs6)
+        list4 = load_list("list4", offs4)
+        list3 = load_list("list3", offs3)
+        list5 = load_list("list5", offs5)
+        row_vals = []
+        for name, src in (("slope", sp), ("offset", bo), ("weight", so)):
+            t = tile(name, [P, 2], F32)
+            with nc.allow_non_contiguous_dma(reason="one value a partition"):
+                nc.sync.dma_start(t[:], src.rearrange("(h p) o -> p (h o)", p=P))
+            row_vals.append(t)
+        slope, offset, weight = row_vals
+
+        page_w = [tile("page_w%d" % h, [P, E], F32) for h in range(2)]
+        page_v = [tile("page_v%d" % h, [P, E], F32) for h in range(2)]
+        for page in page_v + page_w:
+            nc.vector.memset(page[:], 0.0)
+
+        for q in range(4):
+            nc.vector.tensor_copy(w_planes_raw[32 * q : 32 * q + 4, :].bitcast(I32), w_stage[:, q, :].bitcast(I32))
+        s1 = tile("s1", [P, J], U8)
+        nc.vector.tensor_copy(s1[:], x_plane[:].indirect(list1[:]))
+        w_planes = tile("w_planes", [P, 2 * R], U8)
+        nc.vector.tensor_copy(
+            w_planes[:].rearrange("p (i t m) -> p i m t", i=2, t=PACK),
+            w_planes_raw[:].rearrange("p (i m t) -> p i m t", i=2, t=PACK),
+        )
+        w_codes = tile("w_codes", [P, 2 * R], U8)
+        nc.scalar.copy(
+            w_codes[:].bitcast(U16).rearrange("p (t m) -> p m t", t=PACK),
+            w_raw[:].bitcast(U16).rearrange("p (m t) -> p m t", t=PACK),
+        )
+        w2_codes = tile("w2_codes", [P, R], U32)
+        nc.scalar.copy(
+            w2_codes[:].rearrange("p (t m) -> p m t", t=PACK),
+            w2_raw[:].rearrange("p (m t) -> p m t", t=PACK),
+        )
+
+        g1 = [tile("g1_%d" % c, [P, HALF], U32) for c in range(2)]
+        g2 = [tile("g2_%d" % c, [P, HALF], U32) for c in range(2)]
+        s2 = tile("s2", [P, J], U8)
+        for c in range(2):
+            nc.vector.tensor_copy(g1[c][:], x_words[:].indirect(list1[:, c * LIST_COLS : (c + 1) * LIST_COLS]))
+        nc.vector.tensor_copy(s2[:], x_plane[:].indirect(list2[:]))
+        for c in range(2):
+            nc.vector.tensor_copy(g2[c][:], x_words[:].indirect(list2[:, c * LIST_COLS : (c + 1) * LIST_COLS]))
+
+        bank_a = [psum.tile([P, PACK, HALF], F32, name="bank_a%d" % c) for c in range(2)]
+        bank_b = [psum.tile([P, PACK, HALF], F32, name="bank_b%d" % c) for c in range(2)]
+        for c in range(2):
+            for t in range(PACK):
+                nc.tensor.matmul_mx(
+                    out=bank_a[c][:, t, :],
+                    lhsT=w_codes[:, 2 * P * t : 2 * P * (t + 1)].bitcast(E2M1),
+                    lhsT_scale=w_planes[:, P * t : P * (t + 1)],
+                    rhs=g1[c][:].bitcast(E5M2),
+                    rhs_scale=s1[:, c * HALF : (c + 1) * HALF],
+                    start=True, stop=True,
+                )
+        for c in range(2):
+            for t in range(PACK):
+                nc.tensor.matmul_mx(
+                    out=bank_b[c][:, t, :],
+                    lhsT=w2_codes[:, P * t : P * (t + 1)].bitcast(E4M3),
+                    lhsT_scale=w_planes[:, R + P * t : R + P * (t + 1)],
+                    rhs=g2[c][:].bitcast(E5M2),
+                    rhs_scale=s2[:, c * HALF : (c + 1) * HALF],
+                    start=True, stop=True,
+                )
+
+        a_sb = [tile("a_sb%d" % c, [P, HALF, PACK], F32) for c in range(2)]
+        diff = [tile("diff%d" % c, [P, HALF, PACK], F32) for c in range(2)]
+        hid = [tile("hid%d" % c, [P, HALF * PACK], BF16) for c in range(2)]
+        hid_codes = [tile("hid_codes%d" % c, [P, HALF], U32) for c in range(2)]
+        hid_plane = [tile("hid_plane%d" % c, [P, HALF], U8) for c in range(2)]
+        for c in range(2):
+            nc.scalar.copy(a_sb[c][:], bank_a[c][:].rearrange("p t j -> p j t"))
+        QUARTER = HALF // 2
+        for c in range(2):
+            for j0 in (0, QUARTER):
+                js = slice(j0, j0 + QUARTER)
+                nc.vector.tensor_tensor(
+                    diff[c][:, js, :], bank_b[c][:, :, js].rearrange("p t j -> p j t"), a_sb[c][:, js, :], ALU.subtract
+                )
+                nc.scalar.activation(
+                    hid[c][:, PACK * j0 : PACK * (j0 + QUARTER)], diff[c][:, js, :].rearrange("p j t -> p (j t)"), ACT.Abs
+                )
+        for c in range(2):
+            nc.vector.quantize_mx(out=hid_codes[c][:].bitcast(E4M3), scales=hid_plane[c][:], in_=hid[c][:])
+
+        bank_p = [psum.tile([P, 2, HALF], F32, name="bank_p%d" % c) for c in range(2)]
+        bank_q = [psum.tile([P, 2, HALF], F32, name="bank_q%d" % c) for c in range(2)]
+        p_sb = [sb.tile([P, J], F32, name="p_sb%d" % h, tag="p%d" % h, align_bytes=64) for h in range(2)]
+        q_first = tile("q_first", [P, 2, HALF], F32)
+        q_low = tile("q_low", [P, HALF], F32)
+        for c in range(2):
+            for h in range(2):
+                nc.tensor.matmul_mx(
+                    out=bank_p[c][:, h, :],
+                    lhsT=wb_codes[:, 2 * P * h : 2 * P * (h + 1)].bitcast(E2M1),
+                    lhsT_scale=wb_plane[:, P * h : P * (h + 1)],
+                    rhs=hid_codes[c][:].bitcast(E4M3),
+                    rhs_scale=hid_plane[c][:],
+                    start=True, stop=True,
+                )
+            for h in range(2):
+                nc.tensor.matmul_mx(
+                    out=bank_q[c][:, h, :],
+                    lhsT=wc_codes[:, P * h : P * (h + 1)].bitcast(E4M3),
+                    lhsT_scale=wc_plane[:, P * h : P * (h + 1)],
+                    rhs=hid_codes[c][:].bitcast(E4M3),
+                    rhs_scale=hid_plane[c][:],
+                    start=True, stop=True,
+                )
+            for h in range(2):
+                nc.scalar.copy(p_sb[h][:, c * HALF : (c + 1) * HALF], bank_p[c][:, h, :])
+            if c == 0:
+                nc.vector.tensor_copy(q_first[:], bank_q[0][:])
+            else:
+                nc.vector.tensor_copy(q_low[:], bank_q[1][:, 0, :])
+
+        gate = [tile("gate%d" % h, [P, U], F32) for h in range(2)]
+        val = [tile("val%d" % h, [P, U], F32) for h in range(2)]
+        res = [tile("res%d" % h, [P, E], F32) for h in range(2)]
+        for h in range(2):
+            nc.scalar.activation(
+                gate[h][:], p_sb[h][:].indirect(list4[:]), ACT.Sigmoid,
+                bias=offset[:, h : h + 1], scale=slope[:, h : h + 1],
+            )
+            nc.scalar.activation(val[h][:], p_sb[h][:].indirect(list3[:]), ACT.Copy, scale=weight[:, h : h + 1])
+        places = [list6[:, c * LIST_COLS : (c + 1) * LIST_COLS] for c in range(2)]
+        nc.vector.tensor_copy(page_v[0][:].indirect(places[0]), q_first[:, 0, :])
+        nc.scalar.activation(page_v[1][:].indirect(places[0]), q_first[:, 1, :], ACT.Copy)
+        nc.vector.tensor_copy(page_v[0][:].indirect(places[1]), q_low[:])
+        q_high = sb.tile([P, HALF], F32, name="q_high", tag="p0", align_bytes=64)
+        nc.scalar.copy(q_high[:], bank_q[1][:, 1, :])
+        nc.scalar.activation(page_v[1][:].indirect(places[1]), q_high[:], ACT.Copy)
+        for h in range(2):
+            nc.vector.tensor_tensor(page_w[h][:].indirect(list5[:]), val[h][:], gate[h][:], ALU.mult)
+            for cols in ([slice(0, E)] if h == 0 else [slice(0, E // 2), slice(E // 2, E)]):
+                nc.vector.tensor_tensor(res[h][:, cols], page_w[h][:, cols], page_v[h][:, cols], ALU.add)
+                nc.sync.dma_start(out[P * h : P * (h + 1), cols], res[h][:, cols])

@@ -31,6 +31,7 @@ def tile_list_outcomegatedpages_ahead_kernel(
     with ExitStack() as ctx:
         lists = ctx.enter_context(tc.tile_pool(name="lists", bufs=1))
         sb = ctx.enter_context(tc.tile_pool(name="sb", bufs=1))
+        shared = ctx.enter_context(tc.tile_pool(name="shared", bufs=1))
         psum = ctx.enter_context(tc.psum_pool(name="psum", bufs=1))
 
         def tile(name, shape, dtype):
@@ -41,17 +42,23 @@ def tile_list_outcomegatedpages_ahead_kernel(
             nc.sync.dma_start(t[:], src)
             return t
 
+        def load_rows(name, src):
+            t = tile(name, [P, 2], F32)
+            with nc.allow_non_contiguous_dma(reason="one value a partition"):
+                nc.sync.dma_start(t[:], src.rearrange("(h p) o -> p (h o)", p=P))
+            return t
+
         def load_plane(queue, plane, scales):
             for q in range(4):
                 queue.dma_start(plane[32 * q : 32 * q + 4, :].bitcast(I32), scales[0, 4 * q : 4 * q + 4, :].bitcast(I32))
 
         x_plane = tile("x_plane", [P, T], U8)
-        nc.gpsimd.memset(x_plane[:].bitcast(I32), 0)
+        nc.vector.memset(x_plane[:, 0 : T // 2].bitcast(I32), 0)
+        nc.gpsimd.memset(x_plane[:, T // 2 : T].bitcast(I32), 0)
         warm_in = tile("warm_in", [P, 1], F32)
         warm_out = tile("warm_out", [P, 1], F32)
         nc.vector.memset(warm_in[:], 0.0)
         nc.scalar.activation(warm_out[:], warm_in[:], ACT.Sigmoid)
-        load_plane(nc.scalar, x_plane, xt_scales)
 
         w_stage = tile("w_stage", [4, 4, 2 * R], U8)
         for i, scales in enumerate((w_scales, w2_scales)):
@@ -59,85 +66,80 @@ def tile_list_outcomegatedpages_ahead_kernel(
                 w_stage[:, :, i * R : (i + 1) * R].bitcast(I32),
                 scales[0].rearrange("(q r) n -> r q n", r=4).bitcast(I32),
             )
-        list1 = load_list("list1", offs)
-        w_raw = tile("w_raw", [P, 2 * R], U8)
-        nc.gpsimd.dma_start(w_raw[:].bitcast(I32), w_words[0].bitcast(I32))
-        x_words = tile("x_words", [P, T], U32)
-        nc.sync.dma_start(x_words[:].bitcast(I32), xt_words[0].rearrange("p t r -> p (t r)").bitcast(I32))
         list2 = load_list("list2", offs2)
+        x_words = tile("x_words", [P, T], U32)
+        x_src = xt_words[0].rearrange("p t r -> p (t r)").bitcast(I32)
+        nc.sync.dma_start(x_words[:, 0 : T // 2].bitcast(I32), x_src[:, 0 : T // 2])
+        load_plane(nc.sync, x_plane, xt_scales)
+        list1 = load_list("list1", offs)
         w2_raw = tile("w2_raw", [P, R], U32)
         nc.sync.dma_start(w2_raw[:].bitcast(I32), w2_words[0].rearrange("p n r -> p (n r)").bitcast(I32))
+        nc.sync.dma_start(x_words[:, T // 2 : T].bitcast(I32), x_src[:, T // 2 : T])
+        w_raw = tile("w_raw", [P, 2 * R], U8)
+        nc.sync.dma_start(w_raw[:].bitcast(I32), w_words[0].bitcast(I32))
 
         w_planes_raw = tile("w_planes_raw", [P, 2 * R], U8)
         nc.vector.memset(w_planes_raw[:].bitcast(I32), 0)
         wb_plane = tile("wb_plane", [P, N], U8)
         wc_plane = tile("wc_plane", [P, N], U8)
-        nc.vector.memset(wc_plane[:].bitcast(I32), 0)
-        nc.vector.memset(wb_plane[:].bitcast(I32), 0)
-        wb_codes = tile("wb_codes", [P, 2 * N], U8)
-        nc.sync.dma_start(wb_codes[:].bitcast(I32), wb_words[0].bitcast(I32))
+        nc.gpsimd.memset(wc_plane[:].bitcast(I32), 0)
+        nc.gpsimd.memset(wb_plane[:].bitcast(I32), 0)
         wc_codes = tile("wc_codes", [P, N], U32)
         nc.sync.dma_start(wc_codes[:].bitcast(I32), wc_words[0].rearrange("p n r -> p (n r)").bitcast(I32))
+        load_plane(nc.sync, wc_plane, wc_scales)
+        wb_codes = tile("wb_codes", [P, 2 * N], U8)
+        nc.sync.dma_start(wb_codes[:].bitcast(I32), wb_words[0].bitcast(I32))
         load_plane(nc.sync, wb_plane, wb_scales)
-        load_plane(nc.gpsimd, wc_plane, wc_scales)
         list6 = load_list("list6", offs6)
         list4 = load_list("list4", offs4)
+        slope = load_rows("slope", sp)
+        offset = load_rows("offset", bo)
         list3 = load_list("list3", offs3)
+        weight = load_rows("weight", so)
         list5 = load_list("list5", offs5)
-        row_vals = []
-        for name, src in (("slope", sp), ("offset", bo), ("weight", so)):
-            t = tile(name, [P, 2], F32)
-            with nc.allow_non_contiguous_dma(reason="one value a partition"):
-                nc.sync.dma_start(t[:], src.rearrange("(h p) o -> p (h o)", p=P))
-            row_vals.append(t)
-        slope, offset, weight = row_vals
 
         page_w = [tile("page_w%d" % h, [P, E], F32) for h in range(2)]
         page_v = [tile("page_v%d" % h, [P, E], F32) for h in range(2)]
         for page in page_v + page_w:
             nc.vector.memset(page[:], 0.0)
 
-        for q in range(4):
+        nc.scalar.copy(w_planes_raw[0:4, :].bitcast(U32), w_stage[:, 0, :].bitcast(U32))
+        for q in range(1, 4):
             nc.vector.tensor_copy(w_planes_raw[32 * q : 32 * q + 4, :].bitcast(I32), w_stage[:, q, :].bitcast(I32))
-        s1 = tile("s1", [P, J], U8)
-        nc.vector.tensor_copy(s1[:], x_plane[:].indirect(list1[:]))
         w_planes = tile("w_planes", [P, 2 * R], U8)
-        nc.vector.tensor_copy(
-            w_planes[:].rearrange("p (i t m) -> p i m t", i=2, t=PACK),
-            w_planes_raw[:].rearrange("p (i m t) -> p i m t", i=2, t=PACK),
+
+        def deal_plane(i):
+            nc.vector.tensor_copy(
+                w_planes[:, i * R : (i + 1) * R].rearrange("p (t m) -> p m t", t=PACK),
+                w_planes_raw[:, i * R : (i + 1) * R].rearrange("p (m t) -> p m t", t=PACK),
+            )
+
+        s1 = tile("s1", [P, J], U8)
+        s2 = tile("s2", [P, J], U8)
+        g1 = [tile("g1_%d" % c, [P, HALF], U32) for c in range(2)]
+        g2 = [tile("g2_%d" % c, [P, HALF], U32) for c in range(2)]
+        nc.vector.tensor_copy(s2[:], x_plane[:].indirect(list2[:]))
+        deal_plane(1)
+        for c in range(2):
+            nc.vector.tensor_copy(g2[c][:], x_words[:].indirect(list2[:, c * LIST_COLS : (c + 1) * LIST_COLS]))
+        deal_plane(0)
+        nc.vector.tensor_copy(s1[:], x_plane[:].indirect(list1[:]))
+        for c in range(2):
+            nc.vector.tensor_copy(g1[c][:], x_words[:].indirect(list1[:, c * LIST_COLS : (c + 1) * LIST_COLS]))
+
+        w2_codes = tile("w2_codes", [P, R], U32)
+        nc.scalar.copy(
+            w2_codes[:].rearrange("p (t m) -> p m t", t=PACK),
+            w2_raw[:].rearrange("p (m t) -> p m t", t=PACK),
         )
         w_codes = tile("w_codes", [P, 2 * R], U8)
         nc.scalar.copy(
             w_codes[:].bitcast(U16).rearrange("p (t m) -> p m t", t=PACK),
             w_raw[:].bitcast(U16).rearrange("p (m t) -> p m t", t=PACK),
         )
-        w2_codes = tile("w2_codes", [P, R], U32)
-        nc.scalar.copy(
-            w2_codes[:].rearrange("p (t m) -> p m t", t=PACK),
-            w2_raw[:].rearrange("p (m t) -> p m t", t=PACK),
-        )
-
-        g1 = [tile("g1_%d" % c, [P, HALF], U32) for c in range(2)]
-        g2 = [tile("g2_%d" % c, [P, HALF], U32) for c in range(2)]
-        s2 = tile("s2", [P, J], U8)
-        for c in range(2):
-            nc.vector.tensor_copy(g1[c][:], x_words[:].indirect(list1[:, c * LIST_COLS : (c + 1) * LIST_COLS]))
-        nc.vector.tensor_copy(s2[:], x_plane[:].indirect(list2[:]))
-        for c in range(2):
-            nc.vector.tensor_copy(g2[c][:], x_words[:].indirect(list2[:, c * LIST_COLS : (c + 1) * LIST_COLS]))
 
         bank_a = [psum.tile([P, PACK, HALF], F32, name="bank_a%d" % c) for c in range(2)]
         bank_b = [psum.tile([P, PACK, HALF], F32, name="bank_b%d" % c) for c in range(2)]
-        for c in range(2):
-            for t in range(PACK):
-                nc.tensor.matmul_mx(
-                    out=bank_a[c][:, t, :],
-                    lhsT=w_codes[:, 2 * P * t : 2 * P * (t + 1)].bitcast(E2M1),
-                    lhsT_scale=w_planes[:, P * t : P * (t + 1)],
-                    rhs=g1[c][:].bitcast(E5M2),
-                    rhs_scale=s1[:, c * HALF : (c + 1) * HALF],
-                    start=True, stop=True,
-                )
         for c in range(2):
             for t in range(PACK):
                 nc.tensor.matmul_mx(
@@ -148,76 +150,85 @@ def tile_list_outcomegatedpages_ahead_kernel(
                     rhs_scale=s2[:, c * HALF : (c + 1) * HALF],
                     start=True, stop=True,
                 )
+        for c in range(2):
+            for t in range(PACK):
+                nc.tensor.matmul_mx(
+                    out=bank_a[c][:, t, :],
+                    lhsT=w_codes[:, 2 * P * t : 2 * P * (t + 1)].bitcast(E2M1),
+                    lhsT_scale=w_planes[:, P * t : P * (t + 1)],
+                    rhs=g1[c][:].bitcast(E5M2),
+                    rhs_scale=s1[:, c * HALF : (c + 1) * HALF],
+                    start=True, stop=True,
+                )
 
-        a_sb = [tile("a_sb%d" % c, [P, HALF, PACK], F32) for c in range(2)]
-        diff = [tile("diff%d" % c, [P, HALF, PACK], F32) for c in range(2)]
-        hid = [tile("hid%d" % c, [P, HALF * PACK], BF16) for c in range(2)]
+        b_sb = [tile("b_sb%d" % c, [P, HALF, PACK], F32) for c in range(2)]
+        QUARTER = HALF // 2
+        diff = [tile("diff%d" % i, [P, QUARTER, PACK], F32) for i in range(3)]
+        diff.append(shared.tile([P, QUARTER, PACK], F32, name="diff3", offset=1024))
+        hid = [sb.tile([P, HALF * PACK], BF16, name="hid%d" % c, tag="hid%d" % c, align_bytes=64) for c in range(2)]
         hid_codes = [tile("hid_codes%d" % c, [P, HALF], U32) for c in range(2)]
         hid_plane = [tile("hid_plane%d" % c, [P, HALF], U8) for c in range(2)]
         for c in range(2):
-            nc.scalar.copy(a_sb[c][:], bank_a[c][:].rearrange("p t j -> p j t"))
-        QUARTER = HALF // 2
+            nc.scalar.copy(b_sb[c][:], bank_b[c][:].rearrange("p t j -> p j t"))
         for c in range(2):
             for j0 in (0, QUARTER):
                 js = slice(j0, j0 + QUARTER)
+                d = diff[2 * c + j0 // QUARTER]
                 nc.vector.tensor_tensor(
-                    diff[c][:, js, :], bank_b[c][:, :, js].rearrange("p t j -> p j t"), a_sb[c][:, js, :], ALU.subtract
+                    d[:], bank_a[c][:, :, js].rearrange("p t j -> p j t"), b_sb[c][:, js, :], ALU.subtract
                 )
                 nc.scalar.activation(
-                    hid[c][:, PACK * j0 : PACK * (j0 + QUARTER)], diff[c][:, js, :].rearrange("p j t -> p (j t)"), ACT.Abs
+                    hid[c][:, PACK * j0 : PACK * (j0 + QUARTER)], d[:].rearrange("p j t -> p (j t)"), ACT.Abs
                 )
         for c in range(2):
             nc.vector.quantize_mx(out=hid_codes[c][:].bitcast(E4M3), scales=hid_plane[c][:], in_=hid[c][:])
 
-        bank_p = [psum.tile([P, 2, HALF], F32, name="bank_p%d" % c) for c in range(2)]
-        bank_q = [psum.tile([P, 2, HALF], F32, name="bank_q%d" % c) for c in range(2)]
-        p_sb = [sb.tile([P, J], F32, name="p_sb%d" % h, tag="p%d" % h, align_bytes=64) for h in range(2)]
-        q_first = tile("q_first", [P, 2, HALF], F32)
-        q_low = tile("q_low", [P, HALF], F32)
-        for c in range(2):
-            for h in range(2):
-                nc.tensor.matmul_mx(
-                    out=bank_p[c][:, h, :],
-                    lhsT=wb_codes[:, 2 * P * h : 2 * P * (h + 1)].bitcast(E2M1),
-                    lhsT_scale=wb_plane[:, P * h : P * (h + 1)],
-                    rhs=hid_codes[c][:].bitcast(E4M3),
-                    rhs_scale=hid_plane[c][:],
-                    start=True, stop=True,
-                )
-            for h in range(2):
-                nc.tensor.matmul_mx(
-                    out=bank_q[c][:, h, :],
-                    lhsT=wc_codes[:, P * h : P * (h + 1)].bitcast(E4M3),
-                    lhsT_scale=wc_plane[:, P * h : P * (h + 1)],
-                    rhs=hid_codes[c][:].bitcast(E4M3),
-                    rhs_scale=hid_plane[c][:],
-                    start=True, stop=True,
-                )
-            for h in range(2):
-                nc.scalar.copy(p_sb[h][:, c * HALF : (c + 1) * HALF], bank_p[c][:, h, :])
-            if c == 0:
-                nc.vector.tensor_copy(q_first[:], bank_q[0][:])
-            else:
-                nc.vector.tensor_copy(q_low[:], bank_q[1][:, 0, :])
-
+        bank_p = [psum.tile([P, J], F32, name="bank_p%d" % h) for h in range(2)]
+        bank_q = [psum.tile([P, J], F32, name="bank_q%d" % h) for h in range(2)]
+        p_sb = [shared.tile([P, J], F32, name="p_sb%d" % h, offset=256 + 1536 * h) for h in range(2)]
+        q_low = [shared.tile([P, HALF], F32, name="q_low0", offset=1280), tile("q_low1", [P, HALF], F32)]
         gate = [tile("gate%d" % h, [P, U], F32) for h in range(2)]
         val = [tile("val%d" % h, [P, U], F32) for h in range(2)]
         res = [tile("res%d" % h, [P, E], F32) for h in range(2)]
+
+        def product(bank, codes, plane, c):
+            nc.tensor.matmul_mx(
+                out=bank[:, c * HALF : (c + 1) * HALF], lhsT=codes, lhsT_scale=plane,
+                rhs=hid_codes[c][:].bitcast(E4M3), rhs_scale=hid_plane[c][:], start=True, stop=True,
+            )
+
+        def product_p(h, c):
+            product(bank_p[h], wb_codes[:, 2 * P * h : 2 * P * (h + 1)].bitcast(E2M1), wb_plane[:, P * h : P * (h + 1)], c)
+
+        def product_q(h, c):
+            product(bank_q[h], wc_codes[:, P * h : P * (h + 1)].bitcast(E4M3), wc_plane[:, P * h : P * (h + 1)], c)
+
+        product_q(0, 0)
+        nc.scalar.copy(q_low[0][:], bank_q[0][:, 0:HALF])
+        for c in range(2):
+            slots = slice(c * HALF, (c + 1) * HALF)
+            for h in range(2):
+                product_p(h, c)
+                nc.scalar.copy(p_sb[h][:, slots], bank_p[h][:, slots])
+            if c == 1:
+                product_q(0, 1)
+            product_q(1, c)
+        nc.vector.tensor_copy(page_v[0][:].indirect(list6[:, 0:LIST_COLS]), q_low[0][:])
+        nc.vector.tensor_copy(q_low[1][:], bank_q[0][:, HALF:J])
+        nc.vector.tensor_copy(page_v[0][:].indirect(list6[:, LIST_COLS : 2 * LIST_COLS]), q_low[1][:])
+
         for h in range(2):
             nc.scalar.activation(
                 gate[h][:], p_sb[h][:].indirect(list4[:]), ACT.Sigmoid,
                 bias=offset[:, h : h + 1], scale=slope[:, h : h + 1],
             )
             nc.scalar.activation(val[h][:], p_sb[h][:].indirect(list3[:]), ACT.Copy, scale=weight[:, h : h + 1])
-        places = [list6[:, c * LIST_COLS : (c + 1) * LIST_COLS] for c in range(2)]
-        nc.vector.tensor_copy(page_v[0][:].indirect(places[0]), q_first[:, 0, :])
-        nc.scalar.activation(page_v[1][:].indirect(places[0]), q_first[:, 1, :], ACT.Copy)
-        nc.vector.tensor_copy(page_v[0][:].indirect(places[1]), q_low[:])
-        q_high = sb.tile([P, HALF], F32, name="q_high", tag="p0", align_bytes=64)
-        nc.scalar.copy(q_high[:], bank_q[1][:, 1, :])
-        nc.scalar.activation(page_v[1][:].indirect(places[1]), q_high[:], ACT.Copy)
+        q_high = shared.tile([P, J], F32, name="q_high", offset=256)
+        nc.vector.tensor_copy(q_high[:], bank_q[1][:])
+        nc.scalar.activation(page_v[1][:].indirect(list6[:]), q_high[:], ACT.Copy)
         for h in range(2):
             nc.vector.tensor_tensor(page_w[h][:].indirect(list5[:]), val[h][:], gate[h][:], ALU.mult)
+        for h in range(2):
             for cols in ([slice(0, E)] if h == 0 else [slice(0, E // 2), slice(E // 2, E)]):
                 nc.vector.tensor_tensor(res[h][:, cols], page_w[h][:, cols], page_v[h][:, cols], ALU.add)
                 nc.sync.dma_start(out[P * h : P * (h + 1), cols], res[h][:, cols])

@@ -31,7 +31,6 @@ def tile_list_outcomegatedpages_ahead_kernel(
     with ExitStack() as ctx:
         lists = ctx.enter_context(tc.tile_pool(name="lists", bufs=1))
         sb = ctx.enter_context(tc.tile_pool(name="sb", bufs=1))
-        shared = ctx.enter_context(tc.tile_pool(name="shared", bufs=1))
         psum = ctx.enter_context(tc.psum_pool(name="psum", bufs=1))
 
         def tile(name, shape, dtype):
@@ -163,8 +162,7 @@ def tile_list_outcomegatedpages_ahead_kernel(
 
         b_sb = [tile("b_sb%d" % c, [P, HALF, PACK], F32) for c in range(2)]
         QUARTER = HALF // 2
-        diff = [tile("diff%d" % i, [P, QUARTER, PACK], F32) for i in range(3)]
-        diff.append(shared.tile([P, QUARTER, PACK], F32, name="diff3", offset=1024))
+        diff = [tile("diff%d" % i, [P, QUARTER, PACK], F32) for i in range(4)]
         hid = [sb.tile([P, HALF * PACK], BF16, name="hid%d" % c, tag="hid%d" % c, align_bytes=64) for c in range(2)]
         hid_codes = [tile("hid_codes%d" % c, [P, HALF], U32) for c in range(2)]
         hid_plane = [tile("hid_plane%d" % c, [P, HALF], U8) for c in range(2)]
@@ -183,48 +181,53 @@ def tile_list_outcomegatedpages_ahead_kernel(
         for c in range(2):
             nc.vector.quantize_mx(out=hid_codes[c][:].bitcast(E4M3), scales=hid_plane[c][:], in_=hid[c][:])
 
-        bank_p = [psum.tile([P, J], F32, name="bank_p%d" % h) for h in range(2)]
-        bank_q = [psum.tile([P, J], F32, name="bank_q%d" % h) for h in range(2)]
-        p_sb = [shared.tile([P, J], F32, name="p_sb%d" % h, offset=256 + 1536 * h) for h in range(2)]
-        q_low = [shared.tile([P, HALF], F32, name="q_low0", offset=1280), tile("q_low1", [P, HALF], F32)]
+        bank_q00 = psum.tile([P, HALF], F32, name="bank_q00")
+        bank_low = psum.tile([P, 3, HALF], F32, name="bank_low")
+        bank_high = psum.tile([P, 4, HALF], F32, name="bank_high")
+        p_psum = [[bank_low[:, 0, :], bank_low[:, 1, :]], [bank_high[:, 0, :], bank_high[:, 1, :]]]
+        q_psum = [[bank_q00[:], bank_low[:, 2, :]], [bank_high[:, 2, :], bank_high[:, 3, :]]]
+        p_sb = [sb.tile([P, J], F32, name="p_sb%d" % h, tag="p%d" % h, align_bytes=64) for h in range(2)]
+        q_low = [sb.tile([P, HALF], F32, name="q_low0", tag="hid1", align_bytes=64), tile("q_low1", [P, HALF], F32)]
         gate = [tile("gate%d" % h, [P, U], F32) for h in range(2)]
         val = [tile("val%d" % h, [P, U], F32) for h in range(2)]
         res = [tile("res%d" % h, [P, E], F32) for h in range(2)]
 
-        def product(bank, codes, plane, c):
+        def product(dst, codes, plane, c):
             nc.tensor.matmul_mx(
-                out=bank[:, c * HALF : (c + 1) * HALF], lhsT=codes, lhsT_scale=plane,
+                out=dst, lhsT=codes, lhsT_scale=plane,
                 rhs=hid_codes[c][:].bitcast(E4M3), rhs_scale=hid_plane[c][:], start=True, stop=True,
             )
 
         def product_p(h, c):
-            product(bank_p[h], wb_codes[:, 2 * P * h : 2 * P * (h + 1)].bitcast(E2M1), wb_plane[:, P * h : P * (h + 1)], c)
+            product(p_psum[h][c], wb_codes[:, 2 * P * h : 2 * P * (h + 1)].bitcast(E2M1), wb_plane[:, P * h : P * (h + 1)], c)
 
         def product_q(h, c):
-            product(bank_q[h], wc_codes[:, P * h : P * (h + 1)].bitcast(E4M3), wc_plane[:, P * h : P * (h + 1)], c)
+            product(q_psum[h][c], wc_codes[:, P * h : P * (h + 1)].bitcast(E4M3), wc_plane[:, P * h : P * (h + 1)], c)
 
-        product_q(0, 0)
-        nc.scalar.copy(q_low[0][:], bank_q[0][:, 0:HALF])
-        for c in range(2):
-            slots = slice(c * HALF, (c + 1) * HALF)
-            for h in range(2):
-                product_p(h, c)
-                nc.scalar.copy(p_sb[h][:, slots], bank_p[h][:, slots])
-            if c == 1:
-                product_q(0, 1)
-            product_q(1, c)
-        nc.vector.tensor_copy(page_v[0][:].indirect(list6[:, 0:LIST_COLS]), q_low[0][:])
-        nc.vector.tensor_copy(q_low[1][:], bank_q[0][:, HALF:J])
-        nc.vector.tensor_copy(page_v[0][:].indirect(list6[:, LIST_COLS : 2 * LIST_COLS]), q_low[1][:])
-
-        for h in range(2):
+        def look(h):
             nc.scalar.activation(
                 gate[h][:], p_sb[h][:].indirect(list4[:]), ACT.Sigmoid,
                 bias=offset[:, h : h + 1], scale=slope[:, h : h + 1],
             )
             nc.scalar.activation(val[h][:], p_sb[h][:].indirect(list3[:]), ACT.Copy, scale=weight[:, h : h + 1])
-        q_high = shared.tile([P, J], F32, name="q_high", offset=256)
-        nc.vector.tensor_copy(q_high[:], bank_q[1][:])
+
+        product_q(0, 0)
+        for c in range(2):
+            product_p(0, c)
+        nc.scalar.copy(p_sb[0][:], bank_low[:, 0:2, :].rearrange("p c j -> p (c j)"))
+        for c in range(2):
+            product_p(1, c)
+        for c in range(2):
+            product_q(1, c)
+        product_q(0, 1)
+        for c in range(2):
+            nc.vector.tensor_copy(q_low[c][:], q_psum[0][c])
+            nc.vector.tensor_copy(page_v[0][:].indirect(list6[:, c * LIST_COLS : (c + 1) * LIST_COLS]), q_low[c][:])
+        look(0)
+        nc.scalar.copy(p_sb[1][:], bank_high[:, 0:2, :].rearrange("p c j -> p (c j)"))
+        look(1)
+        q_high = sb.tile([P, J], F32, name="q_high", tag="p0", align_bytes=64)
+        nc.vector.tensor_copy(q_high[:], bank_high[:, 2:4, :].rearrange("p c j -> p (c j)"))
         nc.scalar.activation(page_v[1][:].indirect(list6[:]), q_high[:], ACT.Copy)
         for h in range(2):
             nc.vector.tensor_tensor(page_w[h][:].indirect(list5[:]), val[h][:], gate[h][:], ALU.mult)

from contextlib import ExitStack

import concourse.mybir as mybir

K, T, J, R, N, U, E = 512, 2048, 256, 512, 256, 128, 512
FLOPS = 2 * (2 * K * R * J + 2 * R * N * J)

F32 = mybir.dt.float32
BF16 = mybir.dt.bfloat16
I32 = mybir.dt.int32
U32 = mybir.dt.uint32
U16 = mybir.dt.uint16
U8 = mybir.dt.uint8
E4M3 = mybir.dt.float8_e4m3fn_x4
E5M2 = mybir.dt.float8_e5m2_x4
E2M1 = mybir.dt.float4_e2m1fn_x4
ACT = mybir.ActivationFunctionType
ALU = mybir.AluOpType

P = 128
PACK = 4
HALF = J // 2
LIST_COLS = HALF // 16


def tile_list_outcomegatedpages_ahead_kernel(
    tc, xt_words, xt_scales, w_words, w_scales, w2_words, w2_scales, wb_words, wb_scales, wc_words, wc_scales,
    so, sp, bo, offs, offs2, offs3, offs4, offs5, offs6, out,
):
    nc = tc.nc
    with ExitStack() as ctx:
        lists = ctx.enter_context(tc.tile_pool(name="lists", bufs=1))
        sb = ctx.enter_context(tc.tile_pool(name="sb", bufs=1))
        psum = ctx.enter_context(tc.psum_pool(name="psum", bufs=1))

        def tile(name, shape, dtype):
            return sb.tile(shape, dtype, name=name, align_bytes=64)

        def load_list(name, src):
            t = lists.tile(list(src.shape), U16, name=name)
            nc.sync.dma_start(t[:], src)
            return t

        def load_rows(name, src):
            t = tile(name, [P, 2], F32)
            with nc.allow_non_contiguous_dma(reason="one value a partition"):
                nc.sync.dma_start(t[:], src.rearrange("(h p) o -> p (h o)", p=P))
            return t

        def load_plane(queue, plane, scales):
            for q in range(4):
                queue.dma_start(plane[32 * q : 32 * q + 4, :].bitcast(I32), scales[0, 4 * q : 4 * q + 4, :].bitcast(I32))

        x_plane = tile("x_plane", [P, T], U8)
        nc.vector.memset(x_plane[:, 0 : T // 2].bitcast(I32), 0)
        nc.gpsimd.memset(x_plane[:, T // 2 : T].bitcast(I32), 0)
        warm_in = tile("warm_in", [P, 1], F32)
        warm_out = tile("warm_out", [P, 1], F32)
        nc.vector.memset(warm_in[:], 0.0)
        nc.scalar.activation(warm_out[:], warm_in[:], ACT.Sigmoid)

        w_stage = tile("w_stage", [4, 4, 2 * R], U8)
        for i, scales in enumerate((w_scales, w2_scales)):
            nc.sync.dma_start(
                w_stage[:, :, i * R : (i + 1) * R].bitcast(I32),
                scales[0].rearrange("(q r) n -> r q n", r=4).bitcast(I32),
            )
        list2 = load_list("list2", offs2)
        x_words = tile("x_words", [P, T], U32)
        x_src = xt_words[0].rearrange("p t r -> p (t r)").bitcast(I32)
        nc.sync.dma_start(x_words[:, 0 : T // 2].bitcast(I32), x_src[:, 0 : T // 2])
        load_plane(nc.sync, x_plane, xt_scales)
        list1 = load_list("list1", offs)
        w2_raw = tile("w2_raw", [P, R], U32)
        nc.sync.dma_start(w2_raw[:].bitcast(I32), w2_words[0].rearrange("p n r -> p (n r)").bitcast(I32))
        nc.sync.dma_start(x_words[:, T // 2 : T].bitcast(I32), x_src[:, T // 2 : T])
        w_raw = tile("w_raw", [P, 2 * R], U8)
        nc.sync.dma_start(w_raw[:].bitcast(I32), w_words[0].bitcast(I32))

        w_planes_raw = tile("w_planes_raw", [P, 2 * R], U8)
        nc.vector.memset(w_planes_raw[:].bitcast(I32), 0)
        wb_plane = tile("wb_plane", [P, N], U8)
        wc_plane = tile("wc_plane", [P, N], U8)
        nc.gpsimd.memset(wc_plane[:].bitcast(I32), 0)
        nc.gpsimd.memset(wb_plane[:].bitcast(I32), 0)
        wc_codes = tile("wc_codes", [P, N], U32)
        nc.sync.dma_start(wc_codes[:].bitcast(I32), wc_words[0].rearrange("p n r -> p (n r)").bitcast(I32))
        load_plane(nc.sync, wc_plane, wc_scales)
        wb_codes = tile("wb_codes", [P, 2 * N], U8)
        nc.sync.dma_start(wb_codes[:].bitcast(I32), wb_words[0].bitcast(I32))
        load_plane(nc.sync, wb_plane, wb_scales)
        list6 = load_list("list6", offs6)
        list4 = load_list("list4", offs4)
        slope = load_rows("slope", sp)
        offset = load_rows("offset", bo)
        list3 = load_list("list3", offs3)
        weight = load_rows("weight", so)
        list5 = load_list("list5", offs5)

        page_w = [tile("page_w%d" % h, [P, E], F32) for h in range(2)]
        page_v = [tile("page_v%d" % h, [P, E], F32) for h in range(2)]
        for page in page_v + page_w:
            nc.vector.memset(page[:], 0.0)

        nc.scalar.copy(w_planes_raw[0:4, :].bitcast(U32), w_stage[:, 0, :].bitcast(U32))
        for q in range(1, 4):
            nc.vector.tensor_copy(w_planes_raw[32 * q : 32 * q + 4, :].bitcast(I32), w_stage[:, q, :].bitcast(I32))
        w_planes = tile("w_planes", [P, 2 * R], U8)

        def deal_plane(i):
            nc.vector.tensor_copy(
                w_planes[:, i * R : (i + 1) * R].rearrange("p (t m) -> p m t", t=PACK),
                w_planes_raw[:, i * R : (i + 1) * R].rearrange("p (m t) -> p m t", t=PACK),
            )

        s1 = tile("s1", [P, J], U8)
        s2 = tile("s2", [P, J], U8)
        g1 = [tile("g1_%d" % c, [P, HALF], U32) for c in range(2)]
        g2 = [tile("g2_%d" % c, [P, HALF], U32) for c in range(2)]
        nc.vector.tensor_copy(s2[:], x_plane[:].indirect(list2[:]))
        deal_plane(1)
        for c in range(2):
            nc.vector.tensor_copy(g2[c][:], x_words[:].indirect(list2[:, c * LIST_COLS : (c + 1) * LIST_COLS]))
        deal_plane(0)
        nc.vector.tensor_copy(s1[:], x_plane[:].indirect(list1[:]))
        for c in range(2):
            nc.vector.tensor_copy(g1[c][:], x_words[:].indirect(list1[:, c * LIST_COLS : (c + 1) * LIST_COLS]))

        w2_codes = tile("w2_codes", [P, R], U32)
        nc.scalar.copy(
            w2_codes[:].rearrange("p (t m) -> p m t", t=PACK),
            w2_raw[:].rearrange("p (m t) -> p m t", t=PACK),
        )
        w_codes = tile("w_codes", [P, 2 * R], U8)
        nc.scalar.copy(
            w_codes[:].bitcast(U16).rearrange("p (t m) -> p m t", t=PACK),
            w_raw[:].bitcast(U16).rearrange("p (m t) -> p m t", t=PACK),
        )

        bank_a = [psum.tile([P, PACK, HALF], F32, name="bank_a%d" % c) for c in range(2)]
        bank_b = [psum.tile([P, PACK, HALF], F32, name="bank_b%d" % c) for c in range(2)]
        for c in range(2):
            for t in range(PACK):
                nc.tensor.matmul_mx(
                    out=bank_b[c][:, t, :],
                    lhsT=w2_codes[:, P * t : P * (t + 1)].bitcast(E4M3),
                    lhsT_scale=w_planes[:, R + P * t : R + P * (t + 1)],
                    rhs=g2[c][:].bitcast(E5M2),
                    rhs_scale=s2[:, c * HALF : (c + 1) * HALF],
                    start=True, stop=True,
                )
        for c in range(2):
            for t in range(PACK):
                nc.tensor.matmul_mx(
                    out=bank_a[c][:, t, :],
                    lhsT=w_codes[:, 2 * P * t : 2 * P * (t + 1)].bitcast(E2M1),
                    lhsT_scale=w_planes[:, P * t : P * (t + 1)],
                    rhs=g1[c][:].bitcast(E5M2),
                    rhs_scale=s1[:, c * HALF : (c + 1) * HALF],
                    start=True, stop=True,
                )

        b_sb = [tile("b_sb%d" % c, [P, HALF, PACK], F32) for c in range(2)]
        QUARTER = HALF // 2
        diff = [tile("diff%d" % i, [P, QUARTER, PACK], F32) for i in range(4)]
        hid = [sb.tile([P, HALF * PACK], BF16, name="hid%d" % c, tag="hid%d" % c, align_bytes=64) for c in range(2)]
        hid_codes = [tile("hid_codes%d" % c, [P, HALF], U32) for c in range(2)]
        hid_plane = [tile("hid_plane%d" % c, [P, HALF], U8) for c in range(2)]
        for c in range(2):
            nc.scalar.copy(b_sb[c][:], bank_b[c][:].rearrange("p t j -> p j t"))
        for c in range(2):
            for j0 in (0, QUARTER):
                js = slice(j0, j0 + QUARTER)
                d = diff[2 * c + j0 // QUARTER]
                nc.vector.tensor_tensor(
                    d[:], bank_a[c][:, :, js].rearrange("p t j -> p j t"), b_sb[c][:, js, :], ALU.subtract
                )
                nc.scalar.activation(
                    hid[c][:, PACK * j0 : PACK * (j0 + QUARTER)], d[:].rearrange("p j t -> p (j t)"), ACT.Abs
                )
        for c in range(2):
            nc.vector.quantize_mx(out=hid_codes[c][:].bitcast(E4M3), scales=hid_plane[c][:], in_=hid[c][:])

        bank_q00 = psum.tile([P, HALF], F32, name="bank_q00")
        bank_low = psum.tile([P, 3, HALF], F32, name="bank_low")
        bank_high = psum.tile([P, 4, HALF], F32, name="bank_high")
        p_psum = [[bank_low[:, 0, :], bank_low[:, 1, :]], [bank_high[:, 0, :], bank_high[:, 1, :]]]
        q_psum = [[bank_q00[:], bank_low[:, 2, :]], [bank_high[:, 2, :], bank_high[:, 3, :]]]
        p_sb = [sb.tile([P, J], F32, name="p_sb%d" % h, tag="p%d" % h, align_bytes=64) for h in range(2)]
        q_low = [sb.tile([P, HALF], F32, name="q_low0", tag="hid1", align_bytes=64), tile("q_low1", [P, HALF], F32)]
        gate = [tile("gate%d" % h, [P, U], F32) for h in range(2)]
        val = [tile("val%d" % h, [P, U], F32) for h in range(2)]
        res = [tile("res%d" % h, [P, E], F32) for h in range(2)]

        def product(dst, codes, plane, c):
            nc.tensor.matmul_mx(
                out=dst, lhsT=codes, lhsT_scale=plane,
                rhs=hid_codes[c][:].bitcast(E4M3), rhs_scale=hid_plane[c][:], start=True, stop=True,
            )

        def product_p(h, c):
            product(p_psum[h][c], wb_codes[:, 2 * P * h : 2 * P * (h + 1)].bitcast(E2M1), wb_plane[:, P * h : P * (h + 1)], c)

        def product_q(h, c):
            product(q_psum[h][c], wc_codes[:, P * h : P * (h + 1)].bitcast(E4M3), wc_plane[:, P * h : P * (h + 1)], c)

        def look(h):
            nc.scalar.activation(
                gate[h][:], p_sb[h][:].indirect(list4[:]), ACT.Sigmoid,
                bias=offset[:, h : h + 1], scale=slope[:, h : h + 1],
            )
            nc.scalar.activation(val[h][:], p_sb[h][:].indirect(list3[:]), ACT.Copy, scale=weight[:, h : h + 1])

        product_q(0, 0)
        for c in range(2):
            product_p(0, c)
        nc.scalar.copy(p_sb[0][:], bank_low[:, 0:2, :].rearrange("p c j -> p (c j)"))
        for c in range(2):
            product_p(1, c)
        for c in range(2):
            product_q(1, c)
        product_q(0, 1)
        for c in range(2):
            nc.vector.tensor_copy(q_low[c][:], q_psum[0][c])
            nc.vector.tensor_copy(page_v[0][:].indirect(list6[:, c * LIST_COLS : (c + 1) * LIST_COLS]), q_low[c][:])
        look(0)
        nc.scalar.copy(p_sb[1][:], bank_high[:, 0:2, :].rearrange("p c j -> p (c j)"))
        look(1)
        q_high = sb.tile([P, J], F32, name="q_high", tag="p0", align_bytes=64)
        nc.vector.tensor_copy(q_high[:], bank_high[:, 2:4, :].rearrange("p c j -> p (c j)"))
        nc.scalar.activation(page_v[1][:].indirect(list6[:]), q_high[:], ACT.Copy)
        for h in range(2):
            nc.vector.tensor_tensor(page_w[h][:].indirect(list5[:]), val[h][:], gate[h][:], ALU.mult)
        for h in range(2):
            for cols in ([slice(0, E)] if h == 0 else [slice(0, E // 2), slice(E // 2, E)]):
                nc.vector.tensor_tensor(res[h][:, cols], page_w[h][:, cols], page_v[h][:, cols], ALU.add)
                nc.sync.dma_start(out[P * h : P * (h + 1), cols], res[h][:, cols])
